import numpy as np
import ml_dtypes


def mxq(x, axis, fmt="e4m3"):
    dtype, down = {"e4m3": (ml_dtypes.float8_e4m3fn, 7), "e5m2": (ml_dtypes.float8_e5m2, 14)}[fmt]
    v = np.moveaxis(np.asarray(x, np.float32).astype(ml_dtypes.bfloat16).astype(np.float64), axis, -1)
    blocks = v.reshape(v.shape[:-1] + (-1, 32))
    amax = np.abs(blocks).max(-1, keepdims=True)
    byte = np.maximum(np.where(amax > 0, np.frexp(amax)[1] - 1 + 127, 0) - down, 1)
    scale = np.exp2(byte - 127.0)
    codes = (blocks / scale).astype(np.float32).astype(dtype).astype(np.float64)
    return np.moveaxis((codes * scale).reshape(v.shape), -1, axis)


WIDE = False


def mx_kscale(k):
    if not WIDE:
        return np.ones(k)
    levels = np.array([10, -10, 5, -5, 0])
    if k % 512:
        return np.exp2(np.random.permutation(np.resize(levels, k // 32))).repeat(32)
    a = np.empty((k // 512, 16))
    for p in range(k // 512):
        a[p, :8] = np.random.permutation(np.resize(levels, 8))
        for g in range(8):
            far = levels[np.abs(levels - a[p, g]) >= 10]
            a[p, g + 8] = far[np.random.randint(len(far))]
    return np.exp2(a.ravel()).repeat(32)


BF16 = ml_dtypes.bfloat16


def bf(x):
    return np.asarray(x, np.float32).astype(BF16)


def f64(x):
    return np.asarray(x).astype(np.float64)


E2M1 = np.array([0.0, 0.5, 1.0, 1.5, 2.0, 3.0, 4.0, 6.0, -0.0, -0.5, -1.0, -1.5, -2.0, -3.0, -4.0, -6.0])


def pack_weight(w, fmt):
    k, n = w.shape
    w = f64(bf(w)).reshape(k // 32, 32, n)
    amax = np.abs(w).max(1)
    if fmt == "e4m3":
        byte = np.frexp(amax)[1] - 1 + 127 - 7
    else:
        mant, ex = np.frexp(amax / 6.0)
        byte = np.where(mant > 0.5, ex, ex - 1) + 127
    byte = np.clip(np.where(amax > 0, byte, 1), 1, 254)
    scaled = (w * np.exp2(127.0 - byte)[:, None, :]).reshape(k, n).astype(np.float32)
    by_word = np.ascontiguousarray(scaled.reshape(k // 512, 128, 4, n).transpose(0, 1, 3, 2))
    if fmt == "e4m3":
        words = by_word.astype(ml_dtypes.float8_e4m3fn).view(np.uint8)
    else:
        c = by_word.astype(ml_dtypes.float4_e2m1fn).view(np.uint8) & 0xF
        words = c[..., 0::2] | (c[..., 1::2] << 4)
    return np.ascontiguousarray(words), np.ascontiguousarray(byte.astype(np.uint8).reshape(k // 512, 16, n))


def unpack_weight(words, scales, fmt):
    g, p, n, _ = words.shape
    if fmt == "e4m3":
        vals = np.ascontiguousarray(words).view(ml_dtypes.float8_e4m3fn).astype(np.float64)
    else:
        nib = np.empty((g, p, n, 4), np.uint8)
        nib[..., 0::2] = words & 0xF
        nib[..., 1::2] = words >> 4
        vals = E2M1[nib]
    vals = vals * np.repeat(np.exp2(scales.astype(np.float64) - 127.0), 8, axis=1)[..., None]
    return vals.transpose(0, 1, 3, 2).reshape(g * 512, n)
def pack4(w):
    words, scales = pack_weight(w, "e2m1")
    return words.reshape(words.shape[0], 128, -1), scales


def unpack4(words, scales):
    return unpack_weight(words.reshape(words.shape[0], 128, -1, 2), scales, "e2m1")


E4M3FN = np.array([(-1.0 if i & 128 else 1.0) * ((1.0 + (i & 7) / 8.0) * 2.0 ** (((i >> 3) & 15) - 7) if i & 120 else (i & 7) * 2.0 ** -9) for i in range(256)])


def e4m3fn_bytes(y):
    return np.clip(np.asarray(y, np.float64), -448.0, 448.0).astype(np.float32).astype(ml_dtypes.float8_e4m3fn).view(np.uint8)


def e4m3fn_values(b):
    return E4M3FN[b]


T, DI, DO, R = 2048, 1024, 1024, 256


def draw0():
    s, t = mx_kscale(T), mx_kscale(DO)
    x = bf((0.3 + np.random.standard_normal((T, DI))) * s[:, None])
    g = bf(np.random.standard_normal((T, DO)) / np.sqrt(T) / s[:, None])
    v = bf((0.5 + np.random.standard_normal((DI, DO))) / np.sqrt(DI))
    m = bf((1.0 + 0.1 * np.random.standard_normal(DO)) * t)
    b = np.random.standard_normal((R, DO)) / np.sqrt(DO) / t[None, :]
    b_words, b_scales = pack4(b.T)
    return {"x": x, "g": g, "v": v, "m": m, "b_words": b_words, "b_scales": b_scales}


def unit_columns(v):
    n = np.sqrt(np.sum(v * v, axis=0))
    u = v / n[None, :]
    return n, u


def core(x, g, v, m, b_words, b_scales):
    n, u = unit_columns(f64(v))
    gw = mxq(f64(x), 0, "e4m3").T @ mxq(f64(g), 0, "e4m3")
    c = np.sum(u * gw, axis=0)
    dv = (f64(m) / n)[None, :] * (gw - u * c[None, :])
    return mxq(dv, 1, "e4m3") @ unpack4(b_words, b_scales)


def setup_inputs():
    drawn = draw0()
    full = np.asarray(drawn['x']).astype(np.float64)
    scale = (np.abs(full).reshape(16, 128, 8, 128).max(axis=(1, 3)) / 448.0).astype(np.float32)
    given = {}
    for key, value in drawn.items():
        if key == 'x':
            given['x_bytes'] = e4m3fn_bytes(full / np.repeat(np.repeat(scale.astype(np.float64), 128, axis=0), 128, axis=1))
            given['x_scale'] = scale
        else:
            given[key] = value
    return given


def reference(x_bytes, x_scale, g, v, m, b_words, b_scales):
    return core(e4m3fn_values(x_bytes) * np.repeat(np.repeat(x_scale.astype(np.float64), 128, axis=0), 128, axis=1), g, v, m, b_words, b_scales)

@@ -1,0 +1,347 @@
+from contextlib import ExitStack
+
+import concourse.mybir as mybir
+from concourse.masks import make_identity
+
+T, DI, DO, R = 2048, 1024, 1024, 256
+FLOPS = 2 * T * DI * DO + 2 * DI * DO * R
+
+F32 = mybir.dt.float32
+BF16 = mybir.dt.bfloat16
+U8 = mybir.dt.uint8
+U32 = mybir.dt.uint32
+I32 = mybir.dt.int32
+FP8 = mybir.dt.float8_e4m3fn
+FP8X4 = mybir.dt.float8_e4m3fn_x4
+FP4X4 = mybir.dt.float4_e2m1fn_x4
+MULT = mybir.AluOpType.mult
+ADD = mybir.AluOpType.add
+POW = mybir.AluOpType.pow
+COPY = mybir.ActivationFunctionType.Copy
+
+P = 128
+
+
+def tile_doradirectiongradienttoloradown_d2p_kernel(tc, x_bytes, x_scale, g, v, m, b_words, b_scales, out):
+    nc = tc.nc
+    with ExitStack() as ctx:
+        sb = ctx.enter_context(tc.tile_pool(name="sb", bufs=1))
+        ps = ctx.enter_context(tc.psum_pool(name="ps", bufs=1))
+        ctx.enter_context(tc.manual_schedule())
+
+        xs = sb.tile([P, 4, 8], F32, name="xs")
+        xs_src = x_scale.rearrange("(q k) b -> k q b", k=4)
+        for k in range(4):
+            nc.scalar.dma_start(out=xs[32 * k : 32 * k + 32, :, :], in_=xs_src[k].partition_broadcast(32))
+        m_sb = sb.tile([P, 2, 4], BF16, name="m_sb")
+        nc.gpsimd.dma_start(out=m_sb[:], in_=m.rearrange("(h p t) -> p h t", p=P, t=4))
+        ident = sb.tile([P, P], F32, name="ident")
+        make_identity(nc, ident[:])
+        neg_half = sb.tile([P, 4], F32, name="neg_half")
+        nc.gpsimd.memset(neg_half[:], -0.5)
+        bsc = sb.tile([P, 2, R], U8, name="bsc", align_bytes=64)
+        nc.gpsimd.memset(bsc[:].rearrange("p h n -> p (h n)").bitcast(I32), 0)
+        for k in range(4):
+            nc.gpsimd.dma_start(
+                out=bsc[32 * k : 32 * k + 4, :, :].bitcast(I32),
+                in_=b_scales[:, 4 * k : 4 * k + 4, :].rearrange("h q n -> q h n").bitcast(I32),
+            )
+
+        x_src = x_bytes.rearrange("(q p j) w -> q p (j w)", p=P, j=4)
+        g_src = g.rearrange("(q p j) (h w) -> q h p j w", p=P, j=4, h=2)
+        xb, gr = [], {}
+
+        def load_g(q, h):
+            raw = sb.tile([P, 4, 512], BF16, name="graw", tag="graw", bufs=6)
+            nc.sync.dma_start(out=raw[:], in_=g_src[q, h])
+            gr[q, h] = raw
+
+        for q in range(4):
+            t = sb.tile([P, 4096], U8, name="xb%d" % q)
+            if q == 0:
+                nc.sync.dma_start(out=t[:, 0:2048], in_=x_src[q][:, 0:2048])
+                nc.sync.dma_start(out=t[:, 2048:4096], in_=x_src[q][:, 2048:4096])
+            else:
+                nc.sync.dma_start(out=t[:], in_=x_src[q])
+            xb.append(t)
+            load_g(q, 0)
+        v_sb = sb.tile([P, 8, DO], BF16, name="v_sb")
+        v_src = v.rearrange("(d p) w -> p d w", p=P)
+        nc.sync.dma_start(out=v_sb[:, 0:4, :], in_=v_src[:, 0:4, :])
+        nc.sync.dma_start(out=v_sb[:, 4:8, :], in_=v_src[:, 4:8, :])
+        load_g(0, 1)
+        load_g(1, 1)
+        bw = sb.tile([P, 2, 2 * R], U8, name="bw", align_bytes=64)
+        nc.sync.dma_start(out=bw[:], in_=b_words.rearrange("h p w -> p h w"))
+
+        xw, xg, xc, xp = {}, {}, {}, {}
+        gg, gc, gp = {}, {}, {}
+
+        def widen(q, half, eng):
+            if q not in xw:
+                xw[q] = sb.tile([P, 4, 1024], BF16, name="xw", tag="xw", bufs=2)
+            flat = xw[q][:].rearrange("p j w -> p (j w)")
+            cols = slice(2048 * half, 2048 * half + 2048)
+            src = xb[q][:, cols].bitcast(FP8)
+            if eng == "s":
+                nc.scalar.copy(out=flat[:, cols], in_=src)
+            else:
+                nc.vector.tensor_copy(out=flat[:, cols], in_=src)
+
+        def x_interleave(q):
+            xg[q] = sb.tile([P, 1024, 4], BF16, name="xg", tag="xg", bufs=2, align_bytes=64)
+            for b in range(8):
+                cols = slice(128 * b, 128 * b + 128)
+                nc.vector.tensor_scalar(
+                    out=xg[q][:, cols, :].rearrange("p (c i) t -> p c t i", i=4),
+                    in0=xw[q][:, :, cols].rearrange("p t (c i) -> p c t i", i=4),
+                    scalar1=xs[:, q, b : b + 1],
+                    scalar2=None,
+                    op0=MULT,
+                )
+
+        def x_quant(q):
+            xc[q] = sb.tile([P, 1024], U32, name="xc%d" % q, align_bytes=64)
+            xp[q] = sb.tile([P, 1024], U8, name="xp%d" % q, align_bytes=64)
+            nc.vector.quantize_mx(
+                out=xc[q][:].bitcast(FP8X4), scales=xp[q][:], in_=xg[q][:].rearrange("p w j -> p (w j)")
+            )
+
+        def g_interleave(q, h, eng):
+            gg[q, h] = sb.tile([P, 2048], BF16, name="gg", tag="gg", bufs=3, align_bytes=64)
+            dst = gg[q, h][:].rearrange("p (t m j) -> p t m j", t=4, j=4)
+            src = gr[q, h][:].rearrange("p j (m t) -> p t m j", t=4)
+            if eng == "s":
+                nc.scalar.copy(out=dst, in_=src)
+            else:
+                nc.vector.tensor_copy(out=dst, in_=src)
+
+        def g_quant(q, h):
+            gc[q, h] = sb.tile([P, 512], U32, name="gc%d%d" % (q, h), align_bytes=64)
+            gp[q, h] = sb.tile([P, 512], U8, name="gp%d%d" % (q, h), align_bytes=64)
+            nc.vector.quantize_mx(out=gc[q, h][:].bitcast(FP8X4), scales=gp[q, h][:], in_=gg[q, h][:])
+
+        gw = {}
+
+        def mm(b, q):
+            h, t = b // 4, b % 4
+            for n in range(2):
+                if q == 0:
+                    gw[b, n] = ps.tile([P, 512], F32, name="gw", tag="gw", bufs=6)
+                nc.tensor.matmul_mx(
+                    out=gw[b, n][:],
+                    lhsT=gc[q, h][:, 128 * t : 128 * t + 128].bitcast(FP8X4),
+                    lhsT_scale=gp[q, h][:, 128 * t : 128 * t + 128],
+                    rhs=xc[q][:, 512 * n : 512 * n + 512].bitcast(FP8X4),
+                    rhs_scale=xp[q][:, 512 * n : 512 * n + 512],
+                    start=(q == 0),
+                    stop=(q == 3),
+                )
+
+        vt = [sb.tile([P, 2, 1024], F32, name="vt%d" % h) for h in range(2)]
+        v_words = v_sb[:].rearrange("p d w -> p (d w)").bitcast(F32)
+
+        def v_turn(h, k, eng):
+            u, dq = k // 2, k % 2
+            pt = ps.tile([P, 4, 128], F32, name="pt", tag="misc", bufs=2)
+            for i in range(4):
+                base = 512 * (4 * dq + i) + 256 * h
+                nc.tensor.transpose(pt[:, i, :], v_words[:, base + u : base + 256 : 2], ident[:])
+            dst = vt[h][:, u, 512 * dq : 512 * dq + 512]
+            src = pt[:].rearrange("p i m -> p (i m)")
+            if eng == "s":
+                nc.scalar.copy(out=dst, in_=src)
+            else:
+                nc.vector.tensor_copy(out=dst, in_=src)
+
+        def v_col(h, t):
+            words = vt[h][:, t // 2, :].bitcast(BF16)
+            return words.rearrange("p (w e) -> p w e", e=2)[:, :, t % 2]
+
+        pn = {}
+
+        def norm_mm(h):
+            pn[h] = ps.tile([P, 4, 128], F32, name="pn", tag="misc", bufs=2)
+            for t in range(4):
+                for d in range(8):
+                    cols = v_sb[:, d, 512 * h + t : 512 * h + 512 : 4]
+                    nc.tensor.matmul(out=pn[h][:, t, :], lhsT=cols, rhs=cols, start=(d == 0), stop=(d == 7))
+
+        alpha, inv2 = {}, {}
+
+        def norms(h):
+            n2 = sb.tile([P, 4], F32, name="n2%d" % h)
+            for t in range(4):
+                scrap = sb.tile([P, 128], F32, name="scrap", tag="scrap", bufs=2)
+                nc.vector.scalar_tensor_tensor(
+                    out=scrap[:],
+                    in0=pn[h][:, t, :],
+                    scalar=1.0,
+                    in1=ident[:],
+                    op0=MULT,
+                    op1=MULT,
+                    accum_out=n2[:, t : t + 1],
+                )
+            rn = sb.tile([P, 4], F32, name="rn%d" % h)
+            nc.gpsimd.tensor_tensor(out=rn[:], in0=n2[:], in1=neg_half[:], op=POW)
+            alpha[h] = sb.tile([P, 4], F32, name="alpha%d" % h)
+            nc.gpsimd.tensor_tensor(out=alpha[h][:], in0=rn[:], in1=m_sb[:, h, :], op=MULT)
+            inv2[h] = sb.tile([P, 4], F32, name="inv2%d" % h)
+            nc.gpsimd.tensor_tensor(out=inv2[h][:], in0=rn[:], in1=rn[:], op=MULT)
+
+        am, ng, beta = {}, {}, {}
+        dvc, dvg, dvq, dvp = {}, {}, {}, {}
+        for h in range(2):
+            dvq[h] = sb.tile([P, 1024], U32, name="dvq%d" % h, align_bytes=64)
+            dvp[h] = sb.tile([P, 1024], U8, name="dvp%d" % h, align_bytes=64)
+
+        def scale_gw(b):
+            am[b] = sb.tile([P, 1024], F32, name="am", tag="am", bufs=4)
+            for n in range(2):
+                nc.scalar.activation(
+                    out=am[b][:, 512 * n : 512 * n + 512],
+                    in_=gw[b, n][:],
+                    func=COPY,
+                    scale=alpha[b // 4][:, b % 4 : b % 4 + 1],
+                )
+
+        def dot(b):
+            junk = sb.tile([P, 1024], F32, name="junk", tag="junk", bufs=1)
+            ng[b] = sb.tile([P, 1], F32, name="ng%d" % b)
+            nc.vector.scalar_tensor_tensor(
+                out=junk[:],
+                in0=am[b][:],
+                scalar=-1.0,
+                in1=v_col(b // 4, b % 4),
+                op0=MULT,
+                op1=MULT,
+                accum_out=ng[b][:],
+            )
+
+        def make_beta(b):
+            beta[b] = sb.tile([P, 1], F32, name="beta%d" % b)
+            nc.vector.tensor_tensor(out=beta[b][:], in0=ng[b][:], in1=inv2[b // 4][:, b % 4 : b % 4 + 1], op=MULT)
+
+        def dv_cols(b, c0, c1):
+            h, t = b // 4, b % 4
+            if h not in dvc:
+                dvc[h] = sb.tile([P, 4, 1024], BF16, name="dvc", tag="dvc", bufs=2)
+            nc.vector.scalar_tensor_tensor(
+                out=dvc[h][:, t, c0:c1],
+                in0=v_col(h, t)[:, c0:c1],
+                scalar=beta[b][:],
+                in1=am[b][:, c0:c1],
+                op0=MULT,
+                op1=ADD,
+            )
+
+        def dv_interleave(h, n, eng):
+            dvg[h, n] = sb.tile([P, 512, 4], BF16, name="dvg", tag="dvg", bufs=2, align_bytes=64)
+            dst = dvg[h, n][:].rearrange("p (c i) t -> p c t i", i=4)
+            src = dvc[h][:, :, 512 * n : 512 * n + 512].rearrange("p t (c i) -> p c t i", i=4)
+            if eng == "s":
+                nc.scalar.copy(out=dst, in_=src)
+            else:
+                nc.vector.tensor_copy(out=dst, in_=src)
+
+        def dv_quant(h, n):
+            cols = slice(512 * n, 512 * n + 512)
+            nc.vector.quantize_mx(
+                out=dvq[h][:, cols].bitcast(FP8X4),
+                scales=dvp[h][:, cols],
+                in_=dvg[h, n][:].rearrange("p w j -> p (w j)"),
+            )
+
+        out_dst = out.rearrange("(i d p) r -> i p d r", d=2, p=P)
+
+        def finish(i, eng):
+            po = ps.tile([P, 512], F32, name="po", tag="gw", bufs=6)
+            for d in range(2):
+                rows = slice(128 * (2 * i + d), 128 * (2 * i + d) + 128)
+                for n in range(2):
+                    for h in range(2):
+                        nc.tensor.matmul_mx(
+                            out=po[:, 256 * d + 128 * n : 256 * d + 128 * n + 128],
+                            lhsT=dvq[h][:, rows].bitcast(FP8X4),
+                            lhsT_scale=dvp[h][:, rows],
+                            rhs=bw[:, h, 256 * n : 256 * n + 256].bitcast(FP4X4),
+                            rhs_scale=bsc[:, h, 128 * n : 128 * n + 128],
+                            start=(h == 0),
+                            stop=(h == 1),
+                        )
+            res = sb.tile([P, 2, R], F32, name="res", tag="res", bufs=4)
+            flat = res[:].rearrange("p d r -> p (d r)")
+            if eng == "s":
+                nc.scalar.copy(out=flat, in_=po[:])
+            else:
+                nc.vector.tensor_copy(out=flat, in_=po[:])
+            nc.sync.dma_start(out=out_dst[i], in_=res[:])
+
+        for q in range(4):
+            widen(q, 0, "s")
+            widen(q, 1, "s")
+            g_interleave(q, 0, "v" if q == 0 else "s")
+            if q == 2:
+                for k in range(4):
+                    v_turn(0, k, "s")
+                norm_mm(0)
+            x_interleave(q)
+            g_quant(q, 0)
+            x_quant(q)
+            if q == 2:
+                norms(0)
+            for b in range(3):
+                mm(b, q)
+            if q == 0:
+                load_g(2, 1)
+            if q == 1:
+                load_g(3, 1)
+
+        g_interleave(0, 1, "v")
+        g_interleave(1, 1, "v")
+        g_quant(0, 1)
+        for b in range(8):
+            scale_gw(b)
+            if b == 0:
+                for q in range(4):
+                    mm(3, q)
+                norm_mm(1)
+            if b == 1:
+                g_interleave(2, 1, "s")
+            if b == 2:
+                g_interleave(3, 1, "s")
+                v_turn(1, 0, "s")
+                v_turn(1, 1, "s")
+            if b == 3:
+                v_turn(1, 2, "s")
+                v_turn(1, 3, "s")
+            if b == 5:
+                dv_interleave(0, 0, "s")
+            if b == 6:
+                dv_interleave(0, 1, "s")
+            dot(b)
+            if b > 0:
+                dv_cols(b - 1, 0, 1024)
+            if b < 3:
+                g_quant(b + 1, 1)
+            if b == 1:
+                norms(1)
+            if b == 2:
+                for q in range(4):
+                    mm(4, q)
+            if 3 <= b < 6:
+                for q in range(4):
+                    mm(b + 2, q)
+            if b == 6:
+                dv_quant(0, 0)
+            if b == 7:
+                dv_quant(0, 1)
+            make_beta(b)
+        dv_cols(7, 512, 1024)
+        dv_cols(7, 0, 512)
+        dv_interleave(1, 1, "s")
+        dv_interleave(1, 0, "v")
+        dv_quant(1, 0)
+        dv_quant(1, 1)
+        for i in range(4):
+            finish(i, "s" if i % 2 == 0 else "v")

@@ -30,14 +30,11 @@ def tile_doradirectiongradienttoloradown_d2p_kernel(tc, x_bytes, x_scale, g, v, 
         ctx.enter_context(tc.manual_schedule())
 
         xs = sb.tile([P, 4, 8], F32, name="xs")
-        xs_src = x_scale.rearrange("(q k) b -> k q b", k=4)
-        for k in range(4):
-            nc.scalar.dma_start(out=xs[32 * k : 32 * k + 32, :, :], in_=xs_src[k].partition_broadcast(32))
         m_sb = sb.tile([P, 2, 4], BF16, name="m_sb")
         nc.gpsimd.dma_start(out=m_sb[:], in_=m.rearrange("(h p t) -> p h t", p=P, t=4))
         ident = sb.tile([P, P], F32, name="ident")
         make_identity(nc, ident[:])
-        neg_half = sb.tile([P, 4], F32, name="neg_half")
+        neg_half = sb.tile([P, 8], F32, name="neg_half")
         nc.gpsimd.memset(neg_half[:], -0.5)
         bsc = sb.tile([P, 2, R], U8, name="bsc", align_bytes=64)
         nc.gpsimd.memset(bsc[:].rearrange("p h n -> p (h n)").bitcast(I32), 0)
@@ -58,20 +55,30 @@ def tile_doradirectiongradienttoloradown_d2p_kernel(tc, x_bytes, x_scale, g, v, 
 
         for q in range(4):
             t = sb.tile([P, 4096], U8, name="xb%d" % q)
-            if q == 0:
-                nc.sync.dma_start(out=t[:, 0:2048], in_=x_src[q][:, 0:2048])
-                nc.sync.dma_start(out=t[:, 2048:4096], in_=x_src[q][:, 2048:4096])
-            else:
-                nc.sync.dma_start(out=t[:], in_=x_src[q])
             xb.append(t)
-            load_g(q, 0)
         v_sb = sb.tile([P, 8, DO], BF16, name="v_sb")
         v_src = v.rearrange("(d p) w -> p d w", p=P)
+        bw = sb.tile([P, 2, 2 * R], U8, name="bw", align_bytes=64)
+
+        def load_x(q, c0, c1):
+            nc.sync.dma_start(out=xb[q][:, c0:c1], in_=x_src[q][:, c0:c1])
+
+        load_x(0, 0, 2048)
+        load_g(0, 0)
+        load_x(0, 2048, 4096)
+        xs_src = x_scale.rearrange("(q k) b -> k q b", k=4)
+        for k in range(4):
+            nc.sync.dma_start(out=xs[32 * k : 32 * k + 32, :, :], in_=xs_src[k].partition_broadcast(32))
+        load_x(1, 0, 4096)
+        load_g(1, 0)
         nc.sync.dma_start(out=v_sb[:, 0:4, :], in_=v_src[:, 0:4, :])
         nc.sync.dma_start(out=v_sb[:, 4:8, :], in_=v_src[:, 4:8, :])
+        load_x(2, 0, 4096)
+        load_g(2, 0)
+        load_x(3, 0, 4096)
+        load_g(3, 0)
         load_g(0, 1)
         load_g(1, 1)
-        bw = sb.tile([P, 2, 2 * R], U8, name="bw", align_bytes=64)
         nc.sync.dma_start(out=bw[:], in_=b_words.rearrange("h p w -> p h w"))
 
         xw, xg, xc, xp = {}, {}, {}, {}
@@ -108,7 +115,7 @@ def tile_doradirectiongradienttoloradown_d2p_kernel(tc, x_bytes, x_scale, g, v, 
             )
 
         def g_interleave(q, h, eng):
-            gg[q, h] = sb.tile([P, 2048], BF16, name="gg", tag="gg", bufs=3, align_bytes=64)
+            gg[q, h] = sb.tile([P, 2048], BF16, name="gg", tag="gg", bufs=5, align_bytes=64)
             dst = gg[q, h][:].rearrange("p (t m j) -> p t m j", t=4, j=4)
             src = gr[q, h][:].rearrange("p j (m t) -> p t m j", t=4)
             if eng == "s":
@@ -127,7 +134,7 @@ def tile_doradirectiongradienttoloradown_d2p_kernel(tc, x_bytes, x_scale, g, v, 
             h, t = b // 4, b % 4
             for n in range(2):
                 if q == 0:
-                    gw[b, n] = ps.tile([P, 512], F32, name="gw", tag="gw", bufs=6)
+                    gw[b, n] = ps.tile([P, 512], F32, name="gw", tag="gw", bufs=4)
                 nc.tensor.matmul_mx(
                     out=gw[b, n][:],
                     lhsT=gc[q, h][:, 128 * t : 128 * t + 128].bitcast(FP8X4),
@@ -141,14 +148,20 @@ def tile_doradirectiongradienttoloradown_d2p_kernel(tc, x_bytes, x_scale, g, v, 
         vt = [sb.tile([P, 2, 1024], F32, name="vt%d" % h) for h in range(2)]
         v_words = v_sb[:].rearrange("p d w -> p (d w)").bitcast(F32)
 
-        def v_turn(h, k, eng):
+        turned = {}
+
+        def v_turn(h, k):
             u, dq = k // 2, k % 2
-            pt = ps.tile([P, 4, 128], F32, name="pt", tag="misc", bufs=2)
+            pt = ps.tile([P, 4, 128], F32, name="pt", tag="misc", bufs=4)
             for i in range(4):
                 base = 512 * (4 * dq + i) + 256 * h
                 nc.tensor.transpose(pt[:, i, :], v_words[:, base + u : base + 256 : 2], ident[:])
+            turned[h, k] = pt
+
+        def v_keep(h, k, eng):
+            u, dq = k // 2, k % 2
             dst = vt[h][:, u, 512 * dq : 512 * dq + 512]
-            src = pt[:].rearrange("p i m -> p (i m)")
+            src = turned[h, k][:].rearrange("p i m -> p (i m)")
             if eng == "s":
                 nc.scalar.copy(out=dst, in_=src)
             else:
@@ -159,35 +172,59 @@ def tile_doradirectiongradienttoloradown_d2p_kernel(tc, x_bytes, x_scale, g, v, 
             return words.rearrange("p (w e) -> p w e", e=2)[:, :, t % 2]
 
         pn = {}
+        perm = sb.tile([P, 4, 4, 32], F32, name="perm")
+        for k in range(4):
+            nc.vector.tensor_copy(out=perm[:, :, k, :], in_=ident[:].rearrange("p (k t) -> p t k", t=4))
 
         def norm_mm(h):
-            pn[h] = ps.tile([P, 4, 128], F32, name="pn", tag="misc", bufs=2)
-            for t in range(4):
+            pn[h] = ps.tile([P, 4, 128], F32, name="pn", tag="misc", bufs=4)
+            for s in range(4):
                 for d in range(8):
-                    cols = v_sb[:, d, 512 * h + t : 512 * h + 512 : 4]
-                    nc.tensor.matmul(out=pn[h][:, t, :], lhsT=cols, rhs=cols, start=(d == 0), stop=(d == 7))
+                    cols = v_sb[:, d, 512 * h + 128 * s : 512 * h + 128 * s + 128]
+                    nc.tensor.matmul(out=pn[h][:, s, :], lhsT=cols, rhs=cols, start=(d == 0), stop=(d == 7))
 
-        alpha, inv2 = {}, {}
+        n2_nat = sb.tile([P, 8], F32, name="n2_nat")
+        n2 = sb.tile([P, 2, 4], F32, name="n2")
+        rn = sb.tile([P, 2, 4], F32, name="rn")
+        alpha = sb.tile([P, 2, 4], F32, name="alpha")
+        inv2 = sb.tile([P, 2, 4], F32, name="inv2")
 
-        def norms(h):
-            n2 = sb.tile([P, 4], F32, name="n2%d" % h)
-            for t in range(4):
+        def norm_diag(h):
+            for s in range(4):
                 scrap = sb.tile([P, 128], F32, name="scrap", tag="scrap", bufs=2)
                 nc.vector.scalar_tensor_tensor(
                     out=scrap[:],
-                    in0=pn[h][:, t, :],
+                    in0=pn[h][:, s, :],
                     scalar=1.0,
                     in1=ident[:],
                     op0=MULT,
                     op1=MULT,
-                    accum_out=n2[:, t : t + 1],
+                    accum_out=n2_nat[:, 4 * h + s : 4 * h + s + 1],
                 )
-            rn = sb.tile([P, 4], F32, name="rn%d" % h)
-            nc.gpsimd.tensor_tensor(out=rn[:], in0=n2[:], in1=neg_half[:], op=POW)
-            alpha[h] = sb.tile([P, 4], F32, name="alpha%d" % h)
-            nc.gpsimd.tensor_tensor(out=alpha[h][:], in0=rn[:], in1=m_sb[:, h, :], op=MULT)
-            inv2[h] = sb.tile([P, 4], F32, name="inv2%d" % h)
-            nc.gpsimd.tensor_tensor(out=inv2[h][:], in0=rn[:], in1=rn[:], op=MULT)
+
+        pp = []
+
+        def norm_permute():
+            pp.append(ps.tile([P, 4, 8], F32, name="pp", tag="misc", bufs=4))
+            for t in range(4):
+                nc.tensor.matmul(
+                    out=pp[0][:, t, :],
+                    lhsT=perm[:, t, :, :].rearrange("p q k -> p (q k)"),
+                    rhs=n2_nat[:],
+                    start=True,
+                    stop=True,
+                )
+
+        def norm_finish():
+            for k in range(4):
+                rows = slice(32 * k, 32 * k + 32)
+                nc.vector.tensor_copy(
+                    out=n2[rows, :, :], in_=pp[0][rows, :, k:8:4].rearrange("p t h -> p h t")
+                )
+            flat = [a[:].rearrange("p h t -> p (h t)") for a in (n2, rn, alpha, inv2, m_sb)]
+            nc.gpsimd.tensor_tensor(out=flat[1], in0=flat[0], in1=neg_half[:], op=POW)
+            nc.gpsimd.tensor_tensor(out=flat[2], in0=flat[1], in1=flat[4], op=MULT)
+            nc.gpsimd.tensor_tensor(out=flat[3], in0=flat[1], in1=flat[1], op=MULT)
 
         am, ng, beta = {}, {}, {}
         dvc, dvg, dvq, dvp = {}, {}, {}, {}
@@ -202,7 +239,7 @@ def tile_doradirectiongradienttoloradown_d2p_kernel(tc, x_bytes, x_scale, g, v, 
                     out=am[b][:, 512 * n : 512 * n + 512],
                     in_=gw[b, n][:],
                     func=COPY,
-                    scale=alpha[b // 4][:, b % 4 : b % 4 + 1],
+                    scale=alpha[:, b // 4, b % 4 : b % 4 + 1],
                 )
 
         def dot(b):
@@ -220,7 +257,7 @@ def tile_doradirectiongradienttoloradown_d2p_kernel(tc, x_bytes, x_scale, g, v, 
 
         def make_beta(b):
             beta[b] = sb.tile([P, 1], F32, name="beta%d" % b)
-            nc.vector.tensor_tensor(out=beta[b][:], in0=ng[b][:], in1=inv2[b // 4][:, b % 4 : b % 4 + 1], op=MULT)
+            nc.vector.tensor_tensor(out=beta[b][:], in0=ng[b][:], in1=inv2[:, b // 4, b % 4 : b % 4 + 1], op=MULT)
 
         def dv_cols(b, c0, c1):
             h, t = b // 4, b % 4
@@ -255,7 +292,7 @@ def tile_doradirectiongradienttoloradown_d2p_kernel(tc, x_bytes, x_scale, g, v, 
         out_dst = out.rearrange("(i d p) r -> i p d r", d=2, p=P)
 
         def finish(i, eng):
-            po = ps.tile([P, 512], F32, name="po", tag="gw", bufs=6)
+            po = ps.tile([P, 512], F32, name="po", tag="gw", bufs=4)
             for d in range(2):
                 rows = slice(128 * (2 * i + d), 128 * (2 * i + d) + 128)
                 for n in range(2):
@@ -277,68 +314,77 @@ def tile_doradirectiongradienttoloradown_d2p_kernel(tc, x_bytes, x_scale, g, v, 
                 nc.vector.tensor_copy(out=flat, in_=po[:])
             nc.sync.dma_start(out=out_dst[i], in_=res[:])
 
+        v_wide = ((0, 0), (0, 1), (1, 1), (2, 1))
+        v_int = ((3, 0), (1, 1))
         for q in range(4):
-            widen(q, 0, "s")
-            widen(q, 1, "s")
-            g_interleave(q, 0, "v" if q == 0 else "s")
-            if q == 2:
-                for k in range(4):
-                    v_turn(0, k, "s")
-                norm_mm(0)
-            x_interleave(q)
-            g_quant(q, 0)
-            x_quant(q)
-            if q == 2:
-                norms(0)
-            for b in range(3):
-                mm(b, q)
+            if q == 0 and (0, 0) not in v_int:
+                g_interleave(0, 0, "s")
+            for half in range(2):
+                widen(q, half, "v" if (q, half) in v_wide else "s")
+            if q > 0 or (0, 0) in v_int:
+                g_interleave(q, 0, "v" if (q, 0) in v_int else "s")
             if q == 0:
                 load_g(2, 1)
             if q == 1:
                 load_g(3, 1)
-
-        g_interleave(0, 1, "v")
-        g_interleave(1, 1, "v")
-        g_quant(0, 1)
-        for b in range(8):
-            scale_gw(b)
-            if b == 0:
-                for q in range(4):
-                    mm(3, q)
+                norm_mm(0)
                 norm_mm(1)
-            if b == 1:
-                g_interleave(2, 1, "s")
-            if b == 2:
-                g_interleave(3, 1, "s")
-                v_turn(1, 0, "s")
-                v_turn(1, 1, "s")
-            if b == 3:
-                v_turn(1, 2, "s")
-                v_turn(1, 3, "s")
-            if b == 5:
-                dv_interleave(0, 0, "s")
-            if b == 6:
-                dv_interleave(0, 1, "s")
-            dot(b)
-            if b > 0:
-                dv_cols(b - 1, 0, 1024)
-            if b < 3:
-                g_quant(b + 1, 1)
-            if b == 1:
-                norms(1)
-            if b == 2:
-                for q in range(4):
-                    mm(4, q)
-            if 3 <= b < 6:
-                for q in range(4):
-                    mm(b + 2, q)
-            if b == 6:
+            if q == 2:
+                v_turn(0, 0)
+                v_turn(0, 1)
+            if q == 3:
+                norm_permute()
+                v_turn(0, 2)
+                v_turn(0, 3)
+                v_keep(0, 0, "s")
+                v_keep(0, 1, "s")
+            x_interleave(q)
+            if q > 0:
+                x_quant(q - 1)
+                mm(0, q - 1)
+                mm(1, q - 1)
+            if q == 2:
+                norm_diag(0)
+                norm_diag(1)
+            if q == 3:
+                norm_finish()
+            g_quant(q, 0)
+        x_quant(3)
+        mm(0, 3)
+        mm(1, 3)
+        for q in range(4):
+            g_interleave(q, 1, "v" if (q, 1) in v_int else "s")
+            if q == 0:
+                v_keep(0, 2, "s")
+                v_keep(0, 3, "s")
+            g_quant(q, 1)
+        for k in range(4):
+            v_turn(1, k)
+        for c in range(4):
+            scale_gw(2 * c)
+            scale_gw(2 * c + 1)
+            for b in (2 * c + 2, 2 * c + 3):
+                if b < 8:
+                    for q in range(4):
+                        mm(b, q)
+            if c == 0:
+                for k in range(4):
+                    v_keep(1, k, "s")
+            if c >= 2:
+                dv_interleave(0, c - 2, "s")
+            dot(2 * c)
+            dot(2 * c + 1)
+            if c == 3:
                 dv_quant(0, 0)
-            if b == 7:
-                dv_quant(0, 1)
-            make_beta(b)
-        dv_cols(7, 512, 1024)
-        dv_cols(7, 0, 512)
+            make_beta(2 * c)
+            make_beta(2 * c + 1)
+            if c < 3:
+                dv_cols(2 * c, 0, 1024)
+                dv_cols(2 * c + 1, 0, 1024)
+        for n in (1, 0):
+            dv_cols(6, 512 * n, 512 * n + 512)
+            dv_cols(7, 512 * n, 512 * n + 512)
+        dv_quant(0, 1)
         dv_interleave(1, 1, "s")
         dv_interleave(1, 0, "v")
         dv_quant(1, 0)

@@ -115,9 +115,9 @@ def tile_doradirectiongradienttoloradown_d2p_kernel(tc, x_bytes, x_scale, g, v, 
             )
 
         def g_interleave(q, h, eng):
-            gg[q, h] = sb.tile([P, 2048], BF16, name="gg", tag="gg", bufs=5, align_bytes=64)
-            dst = gg[q, h][:].rearrange("p (t m j) -> p t m j", t=4, j=4)
-            src = gr[q, h][:].rearrange("p j (m t) -> p t m j", t=4)
+            gg[q, h] = sb.tile([P, 2048], BF16, name="gg", tag="gg", bufs=4, align_bytes=64)
+            dst = gg[q, h][:].rearrange("p (t m j) -> p m j t", t=4, j=4)
+            src = gr[q, h][:].rearrange("p j (m t) -> p m j t", t=4)
             if eng == "s":
                 nc.scalar.copy(out=dst, in_=src)
             else:
@@ -191,7 +191,7 @@ def tile_doradirectiongradienttoloradown_d2p_kernel(tc, x_bytes, x_scale, g, v, 
 
         def norm_diag(h):
             for s in range(4):
-                scrap = sb.tile([P, 128], F32, name="scrap", tag="scrap", bufs=2)
+                scrap = sb.tile([P, 128], F32, name="scrap", tag="scrap", bufs=4)
                 nc.vector.scalar_tensor_tensor(
                     out=scrap[:],
                     in0=pn[h][:, s, :],
@@ -243,7 +243,7 @@ def tile_doradirectiongradienttoloradown_d2p_kernel(tc, x_bytes, x_scale, g, v, 
                 )
 
         def dot(b):
-            junk = sb.tile([P, 1024], F32, name="junk", tag="junk", bufs=1)
+            junk = sb.tile([P, 1024], F32, name="junk", tag="junk", bufs=2)
             ng[b] = sb.tile([P, 1], F32, name="ng%d" % b)
             nc.vector.scalar_tensor_tensor(
                 out=junk[:],
@@ -358,34 +358,35 @@ def tile_doradirectiongradienttoloradown_d2p_kernel(tc, x_bytes, x_scale, g, v, 
                 v_keep(0, 2, "s")
                 v_keep(0, 3, "s")
             g_quant(q, 1)
+
         for k in range(4):
             v_turn(1, k)
-        for c in range(4):
-            scale_gw(2 * c)
-            scale_gw(2 * c + 1)
-            for b in (2 * c + 2, 2 * c + 3):
-                if b < 8:
-                    for q in range(4):
-                        mm(b, q)
-            if c == 0:
+        for b in range(8):
+            scale_gw(b)
+            if b + 2 < 4:
+                for q in range(4):
+                    mm(b + 2, q)
+            if b == 1:
                 for k in range(4):
                     v_keep(1, k, "s")
-            if c >= 2:
-                dv_interleave(0, c - 2, "s")
-            dot(2 * c)
-            dot(2 * c + 1)
-            if c == 3:
-                dv_quant(0, 0)
-            make_beta(2 * c)
-            make_beta(2 * c + 1)
-            if c < 3:
-                dv_cols(2 * c, 0, 1024)
-                dv_cols(2 * c + 1, 0, 1024)
-        for n in (1, 0):
-            dv_cols(6, 512 * n, 512 * n + 512)
-            dv_cols(7, 512 * n, 512 * n + 512)
-        dv_quant(0, 1)
+            if b == 7:
+                dv_interleave(0, 0, "s")
+                dv_interleave(0, 1, "s")
+            dot(b)
+            if b >= 1:
+                dv_cols(b - 1, 0, 1024)
+            if 4 <= b + 2 < 8:
+                for q in range(4):
+                    mm(b + 2, q)
+            make_beta(b)
+        dv_quant(0, 0)
+        dv_cols(7, 512, 1024)
+        pw = ps.tile([P, 512], F32, name="pw", tag="misc", bufs=4)
+        for i in range(6):
+            nc.tensor.matmul(out=pw[:], lhsT=dvc[1][:, 3, 512:640], rhs=dvc[1][:, 3, 512:1024], start=True, stop=True)
+        dv_cols(7, 0, 512)
         dv_interleave(1, 1, "s")
+        dv_quant(0, 1)
         dv_interleave(1, 0, "v")
         dv_quant(1, 0)
         dv_quant(1, 1)

from contextlib import ExitStack

import concourse.mybir as mybir
from concourse.masks import make_identity

T, DI, DO, R = 2048, 1024, 1024, 256
FLOPS = 2 * T * DI * DO + 2 * DI * DO * R

F32 = mybir.dt.float32
BF16 = mybir.dt.bfloat16
U8 = mybir.dt.uint8
U32 = mybir.dt.uint32
I32 = mybir.dt.int32
FP8 = mybir.dt.float8_e4m3fn
FP8X4 = mybir.dt.float8_e4m3fn_x4
FP4X4 = mybir.dt.float4_e2m1fn_x4
MULT = mybir.AluOpType.mult
ADD = mybir.AluOpType.add
POW = mybir.AluOpType.pow
COPY = mybir.ActivationFunctionType.Copy

P = 128


def tile_doradirectiongradienttoloradown_d2p_kernel(tc, x_bytes, x_scale, g, v, m, b_words, b_scales, out):
    nc = tc.nc
    with ExitStack() as ctx:
        sb = ctx.enter_context(tc.tile_pool(name="sb", bufs=1))
        ps = ctx.enter_context(tc.psum_pool(name="ps", bufs=1))
        ctx.enter_context(tc.manual_schedule())

        xs = sb.tile([P, 4, 8], F32, name="xs")
        m_sb = sb.tile([P, 2, 4], BF16, name="m_sb")
        nc.gpsimd.dma_start(out=m_sb[:], in_=m.rearrange("(h p t) -> p h t", p=P, t=4))
        ident = sb.tile([P, P], F32, name="ident")
        make_identity(nc, ident[:])
        neg_half = sb.tile([P, 8], F32, name="neg_half")
        nc.gpsimd.memset(neg_half[:], -0.5)
        bsc = sb.tile([P, 2, R], U8, name="bsc", align_bytes=64)
        nc.gpsimd.memset(bsc[:].rearrange("p h n -> p (h n)").bitcast(I32), 0)
        for k in range(4):
            nc.gpsimd.dma_start(
                out=bsc[32 * k : 32 * k + 4, :, :].bitcast(I32),
                in_=b_scales[:, 4 * k : 4 * k + 4, :].rearrange("h q n -> q h n").bitcast(I32),
            )

        x_src = x_bytes.rearrange("(q p j) w -> q p (j w)", p=P, j=4)
        g_src = g.rearrange("(q p j) (h w) -> q h p j w", p=P, j=4, h=2)
        xb, gr = [], {}

        def load_g(q, h):
            raw = sb.tile([P, 4, 512], BF16, name="graw", tag="graw", bufs=6)
            nc.sync.dma_start(out=raw[:], in_=g_src[q, h])
            gr[q, h] = raw

        for q in range(4):
            t = sb.tile([P, 4096], U8, name="xb%d" % q)
            xb.append(t)
        v_sb = sb.tile([P, 8, DO], BF16, name="v_sb")
        v_src = v.rearrange("(d p) w -> p d w", p=P)
        bw = sb.tile([P, 2, 2 * R], U8, name="bw", align_bytes=64)

        def load_x(q, c0, c1):
            nc.sync.dma_start(out=xb[q][:, c0:c1], in_=x_src[q][:, c0:c1])

        load_x(0, 0, 2048)
        load_g(0, 0)
        load_x(0, 2048, 4096)
        xs_src = x_scale.rearrange("(q k) b -> k q b", k=4)
        for k in range(4):
            nc.sync.dma_start(out=xs[32 * k : 32 * k + 32, :, :], in_=xs_src[k].partition_broadcast(32))
        load_x(1, 0, 4096)
        load_g(1, 0)
        nc.sync.dma_start(out=v_sb[:, 0:4, :], in_=v_src[:, 0:4, :])
        nc.sync.dma_start(out=v_sb[:, 4:8, :], in_=v_src[:, 4:8, :])
        load_x(2, 0, 4096)
        load_g(2, 0)
        load_x(3, 0, 4096)
        load_g(3, 0)
        load_g(0, 1)
        load_g(1, 1)
        nc.sync.dma_start(out=bw[:], in_=b_words.rearrange("h p w -> p h w"))

        xw, xg, xc, xp = {}, {}, {}, {}
        gg, gc, gp = {}, {}, {}

        def widen(q, half, eng):
            if q not in xw:
                xw[q] = sb.tile([P, 4, 1024], BF16, name="xw", tag="xw", bufs=2)
            flat = xw[q][:].rearrange("p j w -> p (j w)")
            cols = slice(2048 * half, 2048 * half + 2048)
            src = xb[q][:, cols].bitcast(FP8)
            if eng == "s":
                nc.scalar.copy(out=flat[:, cols], in_=src)
            else:
                nc.vector.tensor_copy(out=flat[:, cols], in_=src)

        def x_interleave(q):
            xg[q] = sb.tile([P, 1024, 4], BF16, name="xg", tag="xg", bufs=2, align_bytes=64)
            for b in range(8):
                cols = slice(128 * b, 128 * b + 128)
                nc.vector.tensor_scalar(
                    out=xg[q][:, cols, :].rearrange("p (c i) t -> p c t i", i=4),
                    in0=xw[q][:, :, cols].rearrange("p t (c i) -> p c t i", i=4),
                    scalar1=xs[:, q, b : b + 1],
                    scalar2=None,
                    op0=MULT,
                )

        def x_quant(q):
            xc[q] = sb.tile([P, 1024], U32, name="xc%d" % q, align_bytes=64)
            xp[q] = sb.tile([P, 1024], U8, name="xp%d" % q, align_bytes=64)
            nc.vector.quantize_mx(
                out=xc[q][:].bitcast(FP8X4), scales=xp[q][:], in_=xg[q][:].rearrange("p w j -> p (w j)")
            )

        def g_interleave(q, h, eng):
            gg[q, h] = sb.tile([P, 2048], BF16, name="gg", tag="gg", bufs=4, align_bytes=64)
            dst = gg[q, h][:].rearrange("p (t m j) -> p m j t", t=4, j=4)
            src = gr[q, h][:].rearrange("p j (m t) -> p m j t", t=4)
            if eng == "s":
                nc.scalar.copy(out=dst, in_=src)
            else:
                nc.vector.tensor_copy(out=dst, in_=src)

        def g_quant(q, h):
            gc[q, h] = sb.tile([P, 512], U32, name="gc%d%d" % (q, h), align_bytes=64)
            gp[q, h] = sb.tile([P, 512], U8, name="gp%d%d" % (q, h), align_bytes=64)
            nc.vector.quantize_mx(out=gc[q, h][:].bitcast(FP8X4), scales=gp[q, h][:], in_=gg[q, h][:])

        gw = {}

        def mm(b, q):
            h, t = b // 4, b % 4
            for n in range(2):
                if q == 0:
                    gw[b, n] = ps.tile([P, 512], F32, name="gw", tag="gw", bufs=4)
                nc.tensor.matmul_mx(
                    out=gw[b, n][:],
                    lhsT=gc[q, h][:, 128 * t : 128 * t + 128].bitcast(FP8X4),
                    lhsT_scale=gp[q, h][:, 128 * t : 128 * t + 128],
                    rhs=xc[q][:, 512 * n : 512 * n + 512].bitcast(FP8X4),
                    rhs_scale=xp[q][:, 512 * n : 512 * n + 512],
                    start=(q == 0),
                    stop=(q == 3),
                )

        vt = [sb.tile([P, 2, 1024], F32, name="vt%d" % h) for h in range(2)]
        v_words = v_sb[:].rearrange("p d w -> p (d w)").bitcast(F32)

        turned = {}

        def v_turn(h, k):
            u, dq = k // 2, k % 2
            pt = ps.tile([P, 4, 128], F32, name="pt", tag="misc", bufs=4)
            for i in range(4):
                base = 512 * (4 * dq + i) + 256 * h
                nc.tensor.transpose(pt[:, i, :], v_words[:, base + u : base + 256 : 2], ident[:])
            turned[h, k] = pt

        def v_keep(h, k, eng):
            u, dq = k // 2, k % 2
            dst = vt[h][:, u, 512 * dq : 512 * dq + 512]
            src = turned[h, k][:].rearrange("p i m -> p (i m)")
            if eng == "s":
                nc.scalar.copy(out=dst, in_=src)
            else:
                nc.vector.tensor_copy(out=dst, in_=src)

        def v_col(h, t):
            words = vt[h][:, t // 2, :].bitcast(BF16)
            return words.rearrange("p (w e) -> p w e", e=2)[:, :, t % 2]

        pn = {}
        perm = sb.tile([P, 4, 4, 32], F32, name="perm")
        for k in range(4):
            nc.vector.tensor_copy(out=perm[:, :, k, :], in_=ident[:].rearrange("p (k t) -> p t k", t=4))

        def norm_mm(h):
            pn[h] = ps.tile([P, 4, 128], F32, name="pn", tag="misc", bufs=4)
            for s in range(4):
                for d in range(8):
                    cols = v_sb[:, d, 512 * h + 128 * s : 512 * h + 128 * s + 128]
                    nc.tensor.matmul(out=pn[h][:, s, :], lhsT=cols, rhs=cols, start=(d == 0), stop=(d == 7))

        n2_nat = sb.tile([P, 8], F32, name="n2_nat")
        n2 = sb.tile([P, 2, 4], F32, name="n2")
        rn = sb.tile([P, 2, 4], F32, name="rn")
        alpha = sb.tile([P, 2, 4], F32, name="alpha")
        inv2 = sb.tile([P, 2, 4], F32, name="inv2")

        def norm_diag(h):
            for s in range(4):
                scrap = sb.tile([P, 128], F32, name="scrap", tag="scrap", bufs=4)
                nc.vector.scalar_tensor_tensor(
                    out=scrap[:],
                    in0=pn[h][:, s, :],
                    scalar=1.0,
                    in1=ident[:],
                    op0=MULT,
                    op1=MULT,
                    accum_out=n2_nat[:, 4 * h + s : 4 * h + s + 1],
                )

        pp = []

        def norm_permute():
            pp.append(ps.tile([P, 4, 8], F32, name="pp", tag="misc", bufs=4))
            for t in range(4):
                nc.tensor.matmul(
                    out=pp[0][:, t, :],
                    lhsT=perm[:, t, :, :].rearrange("p q k -> p (q k)"),
                    rhs=n2_nat[:],
                    start=True,
                    stop=True,
                )

        def norm_finish():
            for k in range(4):
                rows = slice(32 * k, 32 * k + 32)
                nc.vector.tensor_copy(
                    out=n2[rows, :, :], in_=pp[0][rows, :, k:8:4].rearrange("p t h -> p h t")
                )
            flat = [a[:].rearrange("p h t -> p (h t)") for a in (n2, rn, alpha, inv2, m_sb)]
            nc.gpsimd.tensor_tensor(out=flat[1], in0=flat[0], in1=neg_half[:], op=POW)
            nc.gpsimd.tensor_tensor(out=flat[2], in0=flat[1], in1=flat[4], op=MULT)
            nc.gpsimd.tensor_tensor(out=flat[3], in0=flat[1], in1=flat[1], op=MULT)

        am, ng, beta = {}, {}, {}
        dvc, dvg, dvq, dvp = {}, {}, {}, {}
        for h in range(2):
            dvq[h] = sb.tile([P, 1024], U32, name="dvq%d" % h, align_bytes=64)
            dvp[h] = sb.tile([P, 1024], U8, name="dvp%d" % h, align_bytes=64)

        def scale_gw(b):
            am[b] = sb.tile([P, 1024], F32, name="am", tag="am", bufs=4)
            for n in range(2):
                nc.scalar.activation(
                    out=am[b][:, 512 * n : 512 * n + 512],
                    in_=gw[b, n][:],
                    func=COPY,
                    scale=alpha[:, b // 4, b % 4 : b % 4 + 1],
                )

        def dot(b):
            junk = sb.tile([P, 1024], F32, name="junk", tag="junk", bufs=2)
            ng[b] = sb.tile([P, 1], F32, name="ng%d" % b)
            nc.vector.scalar_tensor_tensor(
                out=junk[:],
                in0=am[b][:],
                scalar=-1.0,
                in1=v_col(b // 4, b % 4),
                op0=MULT,
                op1=MULT,
                accum_out=ng[b][:],
            )

        def make_beta(b):
            beta[b] = sb.tile([P, 1], F32, name="beta%d" % b)
            nc.vector.tensor_tensor(out=beta[b][:], in0=ng[b][:], in1=inv2[:, b // 4, b % 4 : b % 4 + 1], op=MULT)

        def dv_cols(b, c0, c1):
            h, t = b // 4, b % 4
            if h not in dvc:
                dvc[h] = sb.tile([P, 4, 1024], BF16, name="dvc", tag="dvc", bufs=2)
            nc.vector.scalar_tensor_tensor(
                out=dvc[h][:, t, c0:c1],
                in0=v_col(h, t)[:, c0:c1],
                scalar=beta[b][:],
                in1=am[b][:, c0:c1],
                op0=MULT,
                op1=ADD,
            )

        def dv_interleave(h, n, eng):
            dvg[h, n] = sb.tile([P, 512, 4], BF16, name="dvg", tag="dvg", bufs=2, align_bytes=64)
            dst = dvg[h, n][:].rearrange("p (c i) t -> p c t i", i=4)
            src = dvc[h][:, :, 512 * n : 512 * n + 512].rearrange("p t (c i) -> p c t i", i=4)
            if eng == "s":
                nc.scalar.copy(out=dst, in_=src)
            else:
                nc.vector.tensor_copy(out=dst, in_=src)

        def dv_quant(h, n):
            cols = slice(512 * n, 512 * n + 512)
            nc.vector.quantize_mx(
                out=dvq[h][:, cols].bitcast(FP8X4),
                scales=dvp[h][:, cols],
                in_=dvg[h, n][:].rearrange("p w j -> p (w j)"),
            )

        out_dst = out.rearrange("(i d p) r -> i p d r", d=2, p=P)

        def finish(i, eng):
            po = ps.tile([P, 512], F32, name="po", tag="gw", bufs=4)
            for d in range(2):
                rows = slice(128 * (2 * i + d), 128 * (2 * i + d) + 128)
                for n in range(2):
                    for h in range(2):
                        nc.tensor.matmul_mx(
                            out=po[:, 256 * d + 128 * n : 256 * d + 128 * n + 128],
                            lhsT=dvq[h][:, rows].bitcast(FP8X4),
                            lhsT_scale=dvp[h][:, rows],
                            rhs=bw[:, h, 256 * n : 256 * n + 256].bitcast(FP4X4),
                            rhs_scale=bsc[:, h, 128 * n : 128 * n + 128],
                            start=(h == 0),
                            stop=(h == 1),
                        )
            res = sb.tile([P, 2, R], F32, name="res", tag="res", bufs=4)
            flat = res[:].rearrange("p d r -> p (d r)")
            if eng == "s":
                nc.scalar.copy(out=flat, in_=po[:])
            else:
                nc.vector.tensor_copy(out=flat, in_=po[:])
            nc.sync.dma_start(out=out_dst[i], in_=res[:])

        v_wide = ((0, 0), (0, 1), (1, 1), (2, 1))
        v_int = ((3, 0), (1, 1))
        for q in range(4):
            if q == 0 and (0, 0) not in v_int:
                g_interleave(0, 0, "s")
            for half in range(2):
                widen(q, half, "v" if (q, half) in v_wide else "s")
            if q > 0 or (0, 0) in v_int:
                g_interleave(q, 0, "v" if (q, 0) in v_int else "s")
            if q == 0:
                load_g(2, 1)
            if q == 1:
                load_g(3, 1)
                norm_mm(0)
                norm_mm(1)
            if q == 2:
                v_turn(0, 0)
                v_turn(0, 1)
            if q == 3:
                norm_permute()
                v_turn(0, 2)
                v_turn(0, 3)
                v_keep(0, 0, "s")
                v_keep(0, 1, "s")
            x_interleave(q)
            if q > 0:
                x_quant(q - 1)
                mm(0, q - 1)
                mm(1, q - 1)
            if q == 2:
                norm_diag(0)
                norm_diag(1)
            if q == 3:
                norm_finish()
            g_quant(q, 0)
        x_quant(3)
        mm(0, 3)
        mm(1, 3)
        for q in range(4):
            g_interleave(q, 1, "v" if (q, 1) in v_int else "s")
            if q == 0:
                v_keep(0, 2, "s")
                v_keep(0, 3, "s")
            g_quant(q, 1)

        for k in range(4):
            v_turn(1, k)
        for b in range(8):
            scale_gw(b)
            if b + 2 < 4:
                for q in range(4):
                    mm(b + 2, q)
            if b == 1:
                for k in range(4):
                    v_keep(1, k, "s")
            if b == 7:
                dv_interleave(0, 0, "s")
                dv_interleave(0, 1, "s")
            dot(b)
            if b >= 1:
                dv_cols(b - 1, 0, 1024)
            if 4 <= b + 2 < 8:
                for q in range(4):
                    mm(b + 2, q)
            make_beta(b)
        dv_quant(0, 0)
        dv_cols(7, 512, 1024)
        pw = ps.tile([P, 512], F32, name="pw", tag="misc", bufs=4)
        for i in range(6):
            nc.tensor.matmul(out=pw[:], lhsT=dvc[1][:, 3, 512:640], rhs=dvc[1][:, 3, 512:1024], start=True, stop=True)
        dv_cols(7, 0, 512)
        dv_interleave(1, 1, "s")
        dv_quant(0, 1)
        dv_interleave(1, 0, "v")
        dv_quant(1, 0)
        dv_quant(1, 1)
        for i in range(4):
            finish(i, "s" if i % 2 == 0 else "v")
